import numpy as np
import ml_dtypes


def mxq(x, axis, fmt="e4m3"):
    dtype, down = {"e4m3": (ml_dtypes.float8_e4m3fn, 7), "e5m2": (ml_dtypes.float8_e5m2, 14)}[fmt]
    v = np.moveaxis(np.asarray(x, np.float32).astype(ml_dtypes.bfloat16).astype(np.float64), axis, -1)
    blocks = v.reshape(v.shape[:-1] + (-1, 32))
    amax = np.abs(blocks).max(-1, keepdims=True)
    byte = np.maximum(np.where(amax > 0, np.frexp(amax)[1] - 1 + 127, 0) - down, 1)
    scale = np.exp2(byte - 127.0)
    codes = (blocks / scale).astype(np.float32).astype(dtype).astype(np.float64)
    return np.moveaxis((codes * scale).reshape(v.shape), -1, axis)


WIDE = False


def mx_kscale(k):
    if not WIDE:
        return np.ones(k)
    levels = np.array([10, -10, 5, -5, 0])
    if k % 512:
        return np.exp2(np.random.permutation(np.resize(levels, k // 32))).repeat(32)
    a = np.empty((k // 512, 16))
    for p in range(k // 512):
        a[p, :8] = np.random.permutation(np.resize(levels, 8))
        for g in range(8):
            far = levels[np.abs(levels - a[p, g]) >= 10]
            a[p, g + 8] = far[np.random.randint(len(far))]
    return np.exp2(a.ravel()).repeat(32)


def f64(x):
    return np.asarray(x).astype(np.float64)


def striped(idx):
    return np.tile(idx.reshape(-1, 16).T, (8, 1)).astype(np.uint16)


def unstriped(offs):
    return offs[:16].T.reshape(-1).astype(np.int64)


E2M1 = np.array([0.0, 0.5, 1.0, 1.5, 2.0, 3.0, 4.0, 6.0, -0.0, -0.5, -1.0, -1.5, -2.0, -3.0, -4.0, -6.0])


def pack_weight(w, fmt):
    k, n = w.shape
    w = f64(np.asarray(w, np.float32).astype(ml_dtypes.bfloat16)).reshape(k // 32, 32, n)
    amax = np.abs(w).max(1)
    if fmt == "e4m3":
        byte = np.frexp(amax)[1] - 1 + 127 - 7
    else:
        mant, ex = np.frexp(amax / 6.0)
        byte = np.where(mant > 0.5, ex, ex - 1) + 127
    byte = np.clip(np.where(amax > 0, byte, 1), 1, 254)
    scaled = (w * np.exp2(127.0 - byte)[:, None, :]).reshape(k, n).astype(np.float32)
    by_word = np.ascontiguousarray(scaled.reshape(k // 512, 128, 4, n).transpose(0, 1, 3, 2))
    if fmt == "e4m3":
        words = by_word.astype(ml_dtypes.float8_e4m3fn).view(np.uint8)
    else:
        c = by_word.astype(ml_dtypes.float4_e2m1fn).view(np.uint8) & 0xF
        words = (c[..., 0::2] | (c[..., 1::2] << 4)).reshape(k // 512, 128, 2 * n)
    return np.ascontiguousarray(words), np.ascontiguousarray(byte.astype(np.uint8).reshape(k // 512, 16, n))


def unpack_weight(words, scales, fmt):
    g, _, n = scales.shape
    words = np.ascontiguousarray(words).reshape(g, 128, n, -1)
    if fmt == "e4m3":
        vals = words.view(ml_dtypes.float8_e4m3fn).astype(np.float64)
    else:
        nib = np.empty((g, 128, n, 4), np.uint8)
        nib[..., 0::2] = words & 0xF
        nib[..., 1::2] = words >> 4
        vals = E2M1[nib]
    vals = vals * np.repeat(np.exp2(scales.astype(np.float64) - 127.0), 8, axis=1)[..., None]
    return vals.transpose(0, 1, 3, 2).reshape(g * 512, n)


def gelu(v):
    return 0.5 * v * (1.0 + np.tanh(np.sqrt(2.0 / np.pi) * (v + 0.044715 * v**3)))


K, H, N, T, S, P, P2 = 1536, 512, 768, 2048, 1024, 512, 256

def setup_inputs():
    n = np.random.standard_normal
    s = mx_kscale(K)[:, None]
    u = mx_kscale(H)[:, None]
    tab_words, tab_scales = pack_weight(n((K, T)) * s, "e4m3")
    w1 = 1.3 * n((K, H)) / np.sqrt(K) / s
    w2_words, w2_scales = pack_weight(n((K, H)) / np.sqrt(K) / s * u.T, "e2m1")
    gain = 1.4 * np.exp(0.3 * n(H)) * u[:, 0]
    w3 = n((H, N)) / np.sqrt(H) / u**2
    w4_words, w4_scales = pack_weight(0.8 * n((H, N)) / np.sqrt(H) / u, "e4m3")
    return {
        "tab_words": tab_words, "tab_scales": tab_scales,
        "offs": striped(np.random.permutation(T)[:S]),
        "pos1": striped(np.random.permutation(S)[:P]),
        "pos2": striped(np.random.permutation(S)[:P]),
        "pos3": striped(np.random.permutation(P)[:P2]),
        "pos4": striped(np.random.permutation(P)[:P2]),
        "w1": w1.astype(np.float32),
        "w2_words": w2_words, "w2_scales": w2_scales,
        "gain": gain.astype(np.float32),
        "w3": w3.astype(np.float32),
        "w4_words": w4_words, "w4_scales": w4_scales,
    }

def reference(tab_words, tab_scales, offs, pos1, pos2, pos3, pos4, w1, w2_words, w2_scales, gain, w3, w4_words, w4_scales):
    v = unpack_weight(tab_words, tab_scales, "e4m3")[:, unstriped(offs)]
    w2 = unpack_weight(w2_words, w2_scales, "e2m1")
    w4 = unpack_weight(w4_words, w4_scales, "e4m3")
    h1 = f64(gain)[:, None] * np.tanh(mxq(f64(w1), 0, "e4m3").T @ v)
    h2 = w2.T @ v
    l1, l2 = unstriped(pos1), unstriped(pos2)
    z1 = h1[:, l1] * h1[:, l2]
    z2 = np.abs(h2[:, l1] - h2[:, l2])
    y1 = mxq(f64(w3), 0, "e4m3").T @ mxq(z1, 0, "e4m3")
    y2 = w4.T @ mxq(z2, 0, "e4m3")
    y = np.maximum(y1, y2)
    return y[:, unstriped(pos3)] * y[:, unstriped(pos4)]

@@ -1,0 +1,271 @@
+from contextlib import ExitStack
+
+import concourse.mybir as mybir
+
+K, H, N, T, S, PAIRS, LANES = 1536, 512, 768, 2048, 1024, 512, 256
+FLOPS = 2 * (2 * K * H * S + 2 * H * N * PAIRS)
+
+F32 = mybir.dt.float32
+BF16 = mybir.dt.bfloat16
+I32 = mybir.dt.int32
+U32 = mybir.dt.uint32
+U16 = mybir.dt.uint16
+U8 = mybir.dt.uint8
+FP8X4 = mybir.dt.float8_e4m3fn_x4
+FP4X4 = mybir.dt.float4_e2m1fn_x4
+ACT = mybir.ActivationFunctionType
+ALU = mybir.AluOpType
+
+P = 128
+PACK = 4
+PASSES = K // (P * PACK)
+BANK = 512
+HALVES = S // BANK
+QUADS = 4
+N_TILES = N // P
+W3_CHUNK = 256
+HALF_PAIRS = PAIRS // 2
+
+
+def tile_list_walnut_lane_scores_kernel(
+    tc, tab_words, tab_scales, offs, pos1, pos2, pos3, pos4, w1, w2_words, w2_scales, gain, w3, w4_words, w4_scales, out
+):
+    nc = tc.nc
+    with ExitStack() as ctx:
+        keep = ctx.enter_context(tc.tile_pool(name="keep", bufs=1))
+        ring = ctx.enter_context(tc.tile_pool(name="ring", bufs=3))
+        psum = ctx.enter_context(tc.psum_pool(name="psum", bufs=8))
+
+        def held(name, shape, dtype, tag=None):
+            return keep.tile(shape, dtype, name=name, tag=tag or name, align_bytes=64)
+
+        def load_list(name, source):
+            tile = keep.tile(list(source.shape), U16, name=name)
+            nc.sync.dma_start(tile[:], source)
+            return tile
+
+        idx = load_list("idx", offs)
+        def load_table(a):
+            tile = held(f"table{a}", [P, T], I32)
+            nc.sync.dma_start(tile[:], tab_words[a].rearrange("p t i -> p (t i)").bitcast(I32))
+            return tile
+
+        def load_w1(a):
+            tile = held(f"w1_raw{a}", [P, PACK, H], F32)
+            nc.sync.dma_start(tile[:], w1[a * P * PACK : (a + 1) * P * PACK, :].rearrange("(p j) c -> p j c", j=PACK))
+            return tile
+
+        tab_planes = held("tab_planes", [P, T], U8)
+        nc.vector.memset(tab_planes[:].bitcast(I32), 0)
+        w2_planes_raw = held("w2_planes_raw", [P, PASSES * H], U8)
+        nc.vector.memset(w2_planes_raw[:].bitcast(I32), 0)
+        w4_planes = held("w4_planes", [P, N], U8)
+        nc.vector.memset(w4_planes[:].bitcast(I32), 0)
+        table = [load_table(0)]
+        for q in range(QUADS):
+            nc.scalar.dma_start(
+                tab_planes[32 * q : 32 * q + 4 * PASSES, :].bitcast(I32),
+                tab_scales[:, 4 * q : 4 * q + 4, :].bitcast(I32),
+            )
+        w2_raw = held("w2_raw", [P, PASSES * 2 * H], U8)
+        nc.sync.dma_start(
+            w2_raw[:].bitcast(I32).rearrange("p (a c) -> p a c", a=PASSES),
+            w2_words.bitcast(I32).rearrange("a p c -> p a c"),
+        )
+        for q in range(QUADS):
+            nc.gpsimd.dma_start(
+                w2_planes_raw[32 * q : 32 * q + 4, :].bitcast(I32).rearrange("r (a c) -> r a c", a=PASSES),
+                w2_scales[:, 4 * q : 4 * q + 4, :].bitcast(I32).rearrange("a r c -> r a c"),
+            )
+        w1_raw = [load_w1(0)]
+        table.append(load_table(1))
+        table.append(load_table(2))
+        p1 = load_list("p1", pos1)
+        p2 = load_list("p2", pos2)
+        w1_raw.append(load_w1(1))
+        w1_raw.append(load_w1(2))
+        gains = held("gains", [P, PACK], F32)
+        nc.sync.dma_start(gains[:], gain.rearrange("(p t) -> p t", t=PACK))
+        w3_raw = held("w3_raw", [P, PACK, N], F32)
+        nc.sync.dma_start(w3_raw[:], w3.rearrange("(p j) c -> p j c", j=PACK))
+        w4_codes = held("w4_codes", [P, N], I32)
+        nc.sync.dma_start(w4_codes[:], w4_words[0].rearrange("p c i -> p (c i)").bitcast(I32))
+        for q in range(QUADS):
+            nc.sync.dma_start(
+                w4_planes[32 * q : 32 * q + 4, :].bitcast(I32), w4_scales[0, 4 * q : 4 * q + 4, :].bitcast(I32)
+            )
+        p3 = load_list("p3", pos3)
+        p4 = load_list("p4", pos4)
+
+        picked = [held(f"picked{a}", [P, S], U32) for a in range(PASSES)]
+
+        def pick_words(a, pieces):
+            width = S // pieces
+            for s in range(pieces):
+                nc.vector.tensor_copy(
+                    picked[a][:, s * width : (s + 1) * width],
+                    table[a][:].bitcast(U32).indirect(idx[:, s * width // 16 : (s + 1) * width // 16]),
+                )
+
+        picked_planes = held("picked_planes", [P, S], U8)
+        nc.vector.tensor_copy(picked_planes[:], tab_planes[:].indirect(idx[:]))
+        planes = [picked_planes]
+        live = 32 * (QUADS - 1) + 4
+        for a in range(1, PASSES):
+            shifted = held(f"shifted{a}", [P, S], U8)
+            nc.vector.memset(shifted[:].bitcast(I32), 0)
+            nc.scalar.dma_start(shifted[0:live, :].bitcast(I32), picked_planes[4 * a : 4 * a + live, :].bitcast(I32))
+            planes.append(shifted)
+
+        pick_words(0, 1)
+        w2_codes = held("w2_codes", [P, PASSES * 2 * H], U8)
+        nc.vector.tensor_copy(
+            w2_codes[:].bitcast(U16).rearrange("p (a t m) -> p t a m", a=PASSES, t=PACK),
+            w2_raw[:].bitcast(U16).rearrange("p (a m t) -> p t a m", a=PASSES, t=PACK),
+        )
+        w2_planes = held("w2_planes", [P, PASSES * H], U8)
+        nc.vector.tensor_copy(
+            w2_planes[:].rearrange("p (a t m) -> p t a m", a=PASSES, t=PACK),
+            w2_planes_raw[:].rearrange("p (a m t) -> p t a m", a=PASSES, t=PACK),
+        )
+        pick_words(1, 1)
+        pick_words(2, HALVES)
+
+        w1_codes = [held(f"w1_codes{a}", [P, H], U32) for a in range(PASSES)]
+        w1_planes = [held(f"w1_planes{a}", [P, H], U8) for a in range(PASSES)]
+
+        def quantise_w1(a):
+            dealt = held(f"w1_dealt{a}", [P, PACK * H], BF16)
+            nc.scalar.copy(
+                dealt[:].rearrange("p (t m j) -> p m j t", t=PACK, j=PACK),
+                w1_raw[a][:].rearrange("p j (m t) -> p m j t", t=PACK),
+            )
+            nc.vector.quantize_mx(out=w1_codes[a][:].bitcast(FP8X4), scales=w1_planes[a][:], in_=dealt[:])
+
+        quantise_w1(0)
+        quantise_w1(1)
+
+        banks = {(t, s): psum.tile([P, BANK], F32, name=f"h2_bank{t}{s}", tag="bank") for t in range(PACK) for s in range(HALVES)}
+
+        def h2_passes(t, passes):
+            for a in passes:
+                for s in range(HALVES):
+                    first = a * H + t * P
+                    nc.tensor.matmul_mx(
+                        out=banks[t, s][:],
+                        lhsT=w2_codes[:, 2 * first : 2 * (first + P)].bitcast(FP4X4),
+                        lhsT_scale=w2_planes[:, first : first + P],
+                        rhs=picked[a][:, s * BANK : (s + 1) * BANK].bitcast(FP8X4),
+                        rhs_scale=planes[a][:, s * BANK : (s + 1) * BANK],
+                        start=(a == 0),
+                        stop=(a == PASSES - 1),
+                    )
+
+        for t in range(PACK):
+            h2_passes(t, range(PASSES))
+
+        def combine_pairs(h, dest, op, pieces):
+            width = PAIRS // pieces
+            for s in range(pieces):
+                cols = slice(s * width // 16, (s + 1) * width // 16)
+                second = ring.tile([P, width], F32, name="second", align_bytes=64)
+                nc.vector.tensor_copy(second[:], h[:].indirect(p2[:, cols]))
+                nc.vector.tensor_tensor(dest[:, s * width : (s + 1) * width], h[:].indirect(p1[:, cols]), second[:], op)
+
+        diff = held("diff", [P, PACK, PAIRS], F32)
+        for t in range(PACK):
+            if t == 2:
+                quantise_w1(2)
+            h2 = held(f"h2_{t}", [P, S], F32, tag="w1_raw0" if t == 0 else None)
+            for s in range(HALVES):
+                nc.scalar.copy(h2[:, s * BANK : (s + 1) * BANK], banks[t, s][:])
+            combine_pairs(h2, diff[:, t, :], ALU.subtract, 1)
+
+        prod = held("prod", [P, PACK, PAIRS], F32)
+        for t in range(PACK):
+            bent = ring.tile([P, S], F32, name="bent", bufs=2, align_bytes=64)
+            for s in range(HALVES):
+                bank = psum.tile([P, BANK], F32, name="h1_bank", tag="bank")
+                for a in range(PASSES):
+                    nc.tensor.matmul_mx(
+                        out=bank[:],
+                        lhsT=w1_codes[a][:, t * P : (t + 1) * P].bitcast(FP8X4),
+                        lhsT_scale=w1_planes[a][:, t * P : (t + 1) * P],
+                        rhs=picked[a][:, s * BANK : (s + 1) * BANK].bitcast(FP8X4),
+                        rhs_scale=planes[a][:, s * BANK : (s + 1) * BANK],
+                        start=(a == 0),
+                        stop=(a == PASSES - 1),
+                    )
+                nc.scalar.activation(bent[:, s * BANK : (s + 1) * BANK], bank[:], ACT.Tanh)
+            h1 = held(f"h1_{t}", [P, S], F32)
+            nc.scalar.activation(h1[:], bent[:], ACT.Copy, scale=gains[:, t : t + 1])
+            combine_pairs(h1, prod[:, t, :], ALU.mult, 2 if t == PACK - 1 else 1)
+
+        def interleave(dest, source, func):
+            nc.scalar.activation(
+                dest.rearrange("p (c i t) -> p c t i", i=4, t=PACK), source.rearrange("p t (c i) -> p c t i", i=4), func
+            )
+
+        z2 = held("z2", [P, PACK * PAIRS], BF16)
+        interleave(z2[:], diff[:], ACT.Abs)
+        z2_codes = held("z2_codes", [P, PAIRS], U32)
+        z2_plane = held("z2_plane", [P, PAIRS], U8)
+        nc.vector.quantize_mx(out=z2_codes[:].bitcast(FP8X4), scales=z2_plane[:], in_=z2[:])
+
+        w3_codes, w3_planes = [], []
+
+        def quantise_w3(c):
+            rounded = held(f"w3_rounded{c}", [P, PACK * W3_CHUNK], BF16)
+            interleave(rounded[:], w3_raw[:, :, c * W3_CHUNK : (c + 1) * W3_CHUNK], ACT.Copy)
+            codes = held(f"w3_codes{c}", [P, W3_CHUNK], U32)
+            plane = held(f"w3_plane{c}", [P, W3_CHUNK], U8)
+            nc.vector.quantize_mx(out=codes[:].bitcast(FP8X4), scales=plane[:], in_=rounded[:])
+            w3_codes.append(codes)
+            w3_planes.append(plane)
+
+        quantise_w3(0)
+
+        z1_codes, z1_planes = [], []
+        for s in range(2):
+            z1 = held(f"z1_{s}", [P, PACK * HALF_PAIRS], BF16)
+            interleave(z1[:], prod[:, :, s * HALF_PAIRS : (s + 1) * HALF_PAIRS], ACT.Copy)
+            codes = held(f"z1_codes{s}", [P, HALF_PAIRS], U32)
+            plane = held(f"z1_plane{s}", [P, HALF_PAIRS], U8)
+            nc.vector.quantize_mx(out=codes[:].bitcast(FP8X4), scales=plane[:], in_=z1[:])
+            z1_codes.append(codes)
+            z1_planes.append(plane)
+
+        for n in range(N_TILES):
+            c, at = divmod(n * P, W3_CHUNK)
+            if c == len(w3_codes):
+                quantise_w3(c)
+            y2_bank = psum.tile([P, PAIRS], F32, name="y2_bank", tag="bank")
+            nc.tensor.matmul_mx(
+                out=y2_bank[:],
+                lhsT=w4_codes[:, n * P : (n + 1) * P].bitcast(FP8X4),
+                lhsT_scale=w4_planes[:, n * P : (n + 1) * P],
+                rhs=z2_codes[:].bitcast(FP8X4),
+                rhs_scale=z2_plane[:],
+                start=True,
+                stop=True,
+            )
+            y2 = ring.tile([P, PAIRS], F32, name="y2", align_bytes=64)
+            nc.scalar.copy(y2[:], y2_bank[:])
+            y1_bank = psum.tile([P, PAIRS], F32, name="y1_bank", tag="bank")
+            for s in range(2):
+                nc.tensor.matmul_mx(
+                    out=y1_bank[:, s * HALF_PAIRS : (s + 1) * HALF_PAIRS],
+                    lhsT=w3_codes[c][:, at : at + P].bitcast(FP8X4),
+                    lhsT_scale=w3_planes[c][:, at : at + P],
+                    rhs=z1_codes[s][:].bitcast(FP8X4),
+                    rhs_scale=z1_planes[s][:],
+                    start=True,
+                    stop=True,
+                )
+            y = ring.tile([P, PAIRS], F32, name="y", align_bytes=64)
+            nc.vector.tensor_tensor(y[:], y1_bank[:], y2[:], ALU.max)
+            lane = ring.tile([P, LANES], F32, name="lane", align_bytes=64)
+            nc.vector.tensor_copy(lane[:], y[:].indirect(p4[:]))
+            scores = ring.tile([P, LANES], F32, name="scores", align_bytes=64)
+            nc.vector.tensor_tensor(scores[:], y[:].indirect(p3[:]), lane[:], ALU.mult)
+            nc.sync.dma_start(out[n * P : (n + 1) * P, :], scores[:])

@@ -50,50 +50,44 @@ def tile_list_walnut_lane_scores_kernel(
             nc.sync.dma_start(tile[:], tab_words[a].rearrange("p t i -> p (t i)").bitcast(I32))
             return tile
 
-        def load_w1(a):
-            tile = held(f"w1_raw{a}", [P, PACK, H], F32)
+        def load_w1(a, tag):
+            tile = held(f"w1_raw{a}", [P, PACK, H], F32, tag=tag)
             nc.sync.dma_start(tile[:], w1[a * P * PACK : (a + 1) * P * PACK, :].rearrange("(p j) c -> p j c", j=PACK))
             return tile
 
+        def load_w3(first, last, tag):
+            tile = held(f"w3_raw{first}", [P, PACK, last - first], F32, tag=tag)
+            nc.sync.dma_start(tile[:], w3[:, first:last].rearrange("(p j) c -> p j c", j=PACK))
+            return [tile[:, :, c : c + W3_CHUNK] for c in range(0, last - first, W3_CHUNK)]
+
         tab_planes = held("tab_planes", [P, T], U8)
         nc.vector.memset(tab_planes[:].bitcast(I32), 0)
-        w2_planes_raw = held("w2_planes_raw", [P, PASSES * H], U8)
-        nc.vector.memset(w2_planes_raw[:].bitcast(I32), 0)
-        w4_planes = held("w4_planes", [P, N], U8)
-        nc.vector.memset(w4_planes[:].bitcast(I32), 0)
+        w2_planes = held("w2_planes", [P, PASSES * H], U8)
+        nc.vector.memset(w2_planes[:].bitcast(I32), 0)
         table = [load_table(0)]
         for q in range(QUADS):
             nc.scalar.dma_start(
                 tab_planes[32 * q : 32 * q + 4 * PASSES, :].bitcast(I32),
                 tab_scales[:, 4 * q : 4 * q + 4, :].bitcast(I32),
             )
-        w2_raw = held("w2_raw", [P, PASSES * 2 * H], U8)
-        nc.sync.dma_start(
-            w2_raw[:].bitcast(I32).rearrange("p (a c) -> p a c", a=PASSES),
-            w2_words.bitcast(I32).rearrange("a p c -> p a c"),
-        )
         for q in range(QUADS):
             nc.gpsimd.dma_start(
-                w2_planes_raw[32 * q : 32 * q + 4, :].bitcast(I32).rearrange("r (a c) -> r a c", a=PASSES),
+                w2_planes[32 * q : 32 * q + 4, :].bitcast(I32).rearrange("r (a c) -> r a c", a=PASSES),
                 w2_scales[:, 4 * q : 4 * q + 4, :].bitcast(I32).rearrange("a r c -> r a c"),
             )
-        w1_raw = [load_w1(0)]
         table.append(load_table(1))
+        w3_raw = load_w3(0, W3_CHUNK, None)
         table.append(load_table(2))
+        w2_codes = held("w2_codes", [P, PASSES * 2 * H], U8)
+        nc.sync.dma_start(
+            w2_codes[:].bitcast(I32).rearrange("p (a c) -> p a c", a=PASSES),
+            w2_words.bitcast(I32).rearrange("a p c -> p a c"),
+        )
+        w1_raw = [load_w1(0, None)]
         p1 = load_list("p1", pos1)
         p2 = load_list("p2", pos2)
-        w1_raw.append(load_w1(1))
-        w1_raw.append(load_w1(2))
         gains = held("gains", [P, PACK], F32)
-        nc.sync.dma_start(gains[:], gain.rearrange("(p t) -> p t", t=PACK))
-        w3_raw = held("w3_raw", [P, PACK, N], F32)
-        nc.sync.dma_start(w3_raw[:], w3.rearrange("(p j) c -> p j c", j=PACK))
-        w4_codes = held("w4_codes", [P, N], I32)
-        nc.sync.dma_start(w4_codes[:], w4_words[0].rearrange("p c i -> p (c i)").bitcast(I32))
-        for q in range(QUADS):
-            nc.sync.dma_start(
-                w4_planes[32 * q : 32 * q + 4, :].bitcast(I32), w4_scales[0, 4 * q : 4 * q + 4, :].bitcast(I32)
-            )
+        nc.gpsimd.dma_start(gains[:], gain.rearrange("(p t) -> p t", t=PACK))
         p3 = load_list("p3", pos3)
         p4 = load_list("p4", pos4)
 
@@ -117,33 +111,43 @@ def tile_list_walnut_lane_scores_kernel(
             nc.scalar.dma_start(shifted[0:live, :].bitcast(I32), picked_planes[4 * a : 4 * a + live, :].bitcast(I32))
             planes.append(shifted)
 
+        w1_raw.append(load_w1(1, "tab_planes"))
         pick_words(0, 1)
-        w2_codes = held("w2_codes", [P, PASSES * 2 * H], U8)
-        nc.vector.tensor_copy(
-            w2_codes[:].bitcast(U16).rearrange("p (a t m) -> p t a m", a=PASSES, t=PACK),
-            w2_raw[:].bitcast(U16).rearrange("p (a m t) -> p t a m", a=PASSES, t=PACK),
-        )
-        w2_planes = held("w2_planes", [P, PASSES * H], U8)
-        nc.vector.tensor_copy(
-            w2_planes[:].rearrange("p (a t m) -> p t a m", a=PASSES, t=PACK),
-            w2_planes_raw[:].rearrange("p (a m t) -> p t a m", a=PASSES, t=PACK),
-        )
+        w1_raw.append(load_w1(2, "table0"))
         pick_words(1, 1)
+        w3_raw.extend(load_w3(W3_CHUNK, N, "table1"))
         pick_words(2, HALVES)
 
         w1_codes = [held(f"w1_codes{a}", [P, H], U32) for a in range(PASSES)]
         w1_planes = [held(f"w1_planes{a}", [P, H], U8) for a in range(PASSES)]
 
-        def quantise_w1(a):
+        def quantise_w1(a, copy):
             dealt = held(f"w1_dealt{a}", [P, PACK * H], BF16)
-            nc.scalar.copy(
-                dealt[:].rearrange("p (t m j) -> p m j t", t=PACK, j=PACK),
-                w1_raw[a][:].rearrange("p j (m t) -> p m j t", t=PACK),
+            copy(
+                dealt[:].rearrange("p (t m j) -> p m t j", t=PACK, j=PACK),
+                w1_raw[a][:].rearrange("p j (m t) -> p m t j", t=PACK),
             )
             nc.vector.quantize_mx(out=w1_codes[a][:].bitcast(FP8X4), scales=w1_planes[a][:], in_=dealt[:])
 
-        quantise_w1(0)
-        quantise_w1(1)
+        def interleave(dest, source, copy):
+            copy(dest.rearrange("p (c i t) -> p c t i", i=4, t=PACK), source.rearrange("p t (c i) -> p c t i", i=4))
+
+        def scalar_abs(dest, source):
+            nc.scalar.activation(dest, source, ACT.Abs)
+
+        w3_codes, w3_planes = [], []
+
+        def quantise_w3(c):
+            rounded = held(f"w3_rounded{c}", [P, PACK * W3_CHUNK], BF16)
+            interleave(rounded[:], w3_raw[c], nc.scalar.copy)
+            codes = held(f"w3_codes{c}", [P, W3_CHUNK], U32, tag="table2" if c == 0 else None)
+            plane = held(f"w3_plane{c}", [P, W3_CHUNK], U8)
+            nc.vector.quantize_mx(out=codes[:].bitcast(FP8X4), scales=plane[:], in_=rounded[:])
+            w3_codes.append(codes)
+            w3_planes.append(plane)
+
+        quantise_w3(0)
+        quantise_w1(0, nc.vector.tensor_copy)
 
         banks = {(t, s): psum.tile([P, BANK], F32, name=f"h2_bank{t}{s}", tag="bank") for t in range(PACK) for s in range(HALVES)}
 
@@ -164,22 +168,37 @@ def tile_list_walnut_lane_scores_kernel(
         for t in range(PACK):
             h2_passes(t, range(PASSES))
 
-        def combine_pairs(h, dest, op, pieces):
-            width = PAIRS // pieces
-            for s in range(pieces):
-                cols = slice(s * width // 16, (s + 1) * width // 16)
-                second = ring.tile([P, width], F32, name="second", align_bytes=64)
-                nc.vector.tensor_copy(second[:], h[:].indirect(p2[:, cols]))
-                nc.vector.tensor_tensor(dest[:, s * width : (s + 1) * width], h[:].indirect(p1[:, cols]), second[:], op)
+        def combine_pairs(h, dest, op, tag=None):
+            if tag:
+                second = held("first_second", [P, PAIRS], F32, tag=tag)
+            else:
+                second = ring.tile([P, PAIRS], F32, name="second", align_bytes=64)
+            pieces = [(slice(m, m + HALF_PAIRS), slice(m // 16, (m + HALF_PAIRS) // 16)) for m in (0, HALF_PAIRS)]
+            for pairs, cols in pieces:
+                nc.vector.tensor_copy(second[:, pairs], h[:].indirect(p2[:, cols]))
+            for pairs, cols in pieces:
+                nc.vector.tensor_tensor(dest[:, pairs], h[:].indirect(p1[:, cols]), second[:, pairs], op)
 
-        diff = held("diff", [P, PACK, PAIRS], F32)
+        diff_dealt = held("diff_dealt", [P, PACK, PAIRS], F32)
         for t in range(PACK):
-            if t == 2:
-                quantise_w1(2)
-            h2 = held(f"h2_{t}", [P, S], F32, tag="w1_raw0" if t == 0 else None)
+            if t >= 2:
+                quantise_w1(t - 1, nc.scalar.copy)
+            h2 = held(f"h2_{t}", [P, S], F32, tag={2: "tab_planes", 3: "table0"}.get(t))
             for s in range(HALVES):
                 nc.scalar.copy(h2[:, s * BANK : (s + 1) * BANK], banks[t, s][:])
-            combine_pairs(h2, diff[:, t, :], ALU.subtract, 1)
+            diff = held(f"diff{t}", [P, PAIRS], F32)
+            combine_pairs(h2, diff[:], ALU.subtract, tag="w1_raw0" if t == 0 else None)
+            for i in range(PACK):
+                nc.sync.dma_start(diff_dealt[32 * t : 32 * (t + 1), i, :], diff[i:P:PACK, :])
+
+        w4_codes = held("w4_codes", [P, N], I32, tag="w1_dealt0")
+        nc.sync.dma_start(w4_codes[:], w4_words[0].rearrange("p c i -> p (c i)").bitcast(I32))
+        w4_planes = held("w4_planes", [P, N], U8, tag="w1_dealt1")
+        nc.vector.memset(w4_planes[:].bitcast(I32), 0)
+        for q in range(QUADS):
+            nc.sync.dma_start(
+                w4_planes[32 * q : 32 * q + 4, :].bitcast(I32), w4_scales[0, 4 * q : 4 * q + 4, :].bitcast(I32)
+            )
 
         prod = held("prod", [P, PACK, PAIRS], F32)
         for t in range(PACK):
@@ -199,46 +218,28 @@ def tile_list_walnut_lane_scores_kernel(
                 nc.scalar.activation(bent[:, s * BANK : (s + 1) * BANK], bank[:], ACT.Tanh)
             h1 = held(f"h1_{t}", [P, S], F32)
             nc.scalar.activation(h1[:], bent[:], ACT.Copy, scale=gains[:, t : t + 1])
-            combine_pairs(h1, prod[:, t, :], ALU.mult, 2 if t == PACK - 1 else 1)
-
-        def interleave(dest, source, func):
-            nc.scalar.activation(
-                dest.rearrange("p (c i t) -> p c t i", i=4, t=PACK), source.rearrange("p t (c i) -> p c t i", i=4), func
-            )
+            combine_pairs(h1, prod[:, t, :], ALU.mult)
 
         z2 = held("z2", [P, PACK * PAIRS], BF16)
-        interleave(z2[:], diff[:], ACT.Abs)
+        interleave(z2[:], diff_dealt[:], scalar_abs)
         z2_codes = held("z2_codes", [P, PAIRS], U32)
         z2_plane = held("z2_plane", [P, PAIRS], U8)
         nc.vector.quantize_mx(out=z2_codes[:].bitcast(FP8X4), scales=z2_plane[:], in_=z2[:])
 
-        w3_codes, w3_planes = [], []
-
-        def quantise_w3(c):
-            rounded = held(f"w3_rounded{c}", [P, PACK * W3_CHUNK], BF16)
-            interleave(rounded[:], w3_raw[:, :, c * W3_CHUNK : (c + 1) * W3_CHUNK], ACT.Copy)
-            codes = held(f"w3_codes{c}", [P, W3_CHUNK], U32)
-            plane = held(f"w3_plane{c}", [P, W3_CHUNK], U8)
-            nc.vector.quantize_mx(out=codes[:].bitcast(FP8X4), scales=plane[:], in_=rounded[:])
-            w3_codes.append(codes)
-            w3_planes.append(plane)
-
-        quantise_w3(0)
-
         z1_codes, z1_planes = [], []
         for s in range(2):
             z1 = held(f"z1_{s}", [P, PACK * HALF_PAIRS], BF16)
-            interleave(z1[:], prod[:, :, s * HALF_PAIRS : (s + 1) * HALF_PAIRS], ACT.Copy)
+            interleave(z1[:], prod[:, :, s * HALF_PAIRS : (s + 1) * HALF_PAIRS], nc.vector.tensor_copy if s else nc.scalar.copy)
             codes = held(f"z1_codes{s}", [P, HALF_PAIRS], U32)
             plane = held(f"z1_plane{s}", [P, HALF_PAIRS], U8)
             nc.vector.quantize_mx(out=codes[:].bitcast(FP8X4), scales=plane[:], in_=z1[:])
             z1_codes.append(codes)
             z1_planes.append(plane)
 
-        for n in range(N_TILES):
+        ys, lanes = {}, {}
+
+        def score_views(n):
             c, at = divmod(n * P, W3_CHUNK)
-            if c == len(w3_codes):
-                quantise_w3(c)
             y2_bank = psum.tile([P, PAIRS], F32, name="y2_bank", tag="bank")
             nc.tensor.matmul_mx(
                 out=y2_bank[:],
@@ -262,10 +263,21 @@ def tile_list_walnut_lane_scores_kernel(
                     start=True,
                     stop=True,
                 )
-            y = ring.tile([P, PAIRS], F32, name="y", align_bytes=64)
-            nc.vector.tensor_tensor(y[:], y1_bank[:], y2[:], ALU.max)
-            lane = ring.tile([P, LANES], F32, name="lane", align_bytes=64)
-            nc.vector.tensor_copy(lane[:], y[:].indirect(p4[:]))
-            scores = ring.tile([P, LANES], F32, name="scores", align_bytes=64)
-            nc.vector.tensor_tensor(scores[:], y[:].indirect(p3[:]), lane[:], ALU.mult)
+            ys[n] = ring.tile([P, PAIRS], F32, name="y", bufs=4, align_bytes=64)
+            nc.vector.tensor_tensor(ys[n][:], y1_bank[:], y2[:], ALU.max)
+            if at == 0 and (c + 1) * W3_CHUNK < N:
+                quantise_w3(c + 1)
+
+        def pick_lane(n):
+            lanes[n] = ring.tile([P, LANES], F32, name="lane", align_bytes=64)
+            nc.vector.tensor_copy(lanes[n][:], ys[n][:].indirect(p4[:]))
+
+        def pair_lanes(n):
+            scores = ring.tile([P, LANES], F32, name="scores", bufs=N_TILES, align_bytes=64)
+            nc.vector.tensor_tensor(scores[:], ys[n][:].indirect(p3[:]), lanes[n][:], ALU.mult)
             nc.sync.dma_start(out[n * P : (n + 1) * P, :], scores[:])
+
+        for step in range(N_TILES + 2):
+            for lag, stage in enumerate((score_views, pick_lane, pair_lanes)):
+                if 0 <= step - lag < N_TILES:
+                    stage(step - lag)

@@ -61,35 +61,32 @@ def tile_list_walnut_lane_scores_kernel(
             return [tile[:, :, c : c + W3_CHUNK] for c in range(0, last - first, W3_CHUNK)]
 
         tab_planes = held("tab_planes", [P, T], U8)
-        nc.vector.memset(tab_planes[:].bitcast(I32), 0)
+        nc.gpsimd.memset(tab_planes[:].bitcast(I32), 0)
         w2_planes = held("w2_planes", [P, PASSES * H], U8)
         nc.vector.memset(w2_planes[:].bitcast(I32), 0)
         table = [load_table(0)]
+        p1 = load_list("p1", pos1)
+        p2 = load_list("p2", pos2)
+        p3 = load_list("p3", pos3)
+        p4 = load_list("p4", pos4)
+        w3_raw = load_w3(0, W3_CHUNK, None)
+        table.append(load_table(1))
         for q in range(QUADS):
-            nc.scalar.dma_start(
+            nc.gpsimd.dma_start(
                 tab_planes[32 * q : 32 * q + 4 * PASSES, :].bitcast(I32),
                 tab_scales[:, 4 * q : 4 * q + 4, :].bitcast(I32),
             )
         for q in range(QUADS):
-            nc.gpsimd.dma_start(
+            nc.scalar.dma_start(
                 w2_planes[32 * q : 32 * q + 4, :].bitcast(I32).rearrange("r (a c) -> r a c", a=PASSES),
                 w2_scales[:, 4 * q : 4 * q + 4, :].bitcast(I32).rearrange("a r c -> r a c"),
             )
-        table.append(load_table(1))
-        w3_raw = load_w3(0, W3_CHUNK, None)
         table.append(load_table(2))
         w2_codes = held("w2_codes", [P, PASSES * 2 * H], U8)
         nc.sync.dma_start(
             w2_codes[:].bitcast(I32).rearrange("p (a c) -> p a c", a=PASSES),
             w2_words.bitcast(I32).rearrange("a p c -> p a c"),
         )
-        w1_raw = [load_w1(0, None)]
-        p1 = load_list("p1", pos1)
-        p2 = load_list("p2", pos2)
-        gains = held("gains", [P, PACK], F32)
-        nc.gpsimd.dma_start(gains[:], gain.rearrange("(p t) -> p t", t=PACK))
-        p3 = load_list("p3", pos3)
-        p4 = load_list("p4", pos4)
 
         picked = [held(f"picked{a}", [P, S], U32) for a in range(PASSES)]
 
@@ -111,12 +108,12 @@ def tile_list_walnut_lane_scores_kernel(
             nc.scalar.dma_start(shifted[0:live, :].bitcast(I32), picked_planes[4 * a : 4 * a + live, :].bitcast(I32))
             planes.append(shifted)
 
-        w1_raw.append(load_w1(1, "tab_planes"))
+        w1_raw = [load_w1(0, "tab_planes")]
         pick_words(0, 1)
-        w1_raw.append(load_w1(2, "table0"))
         pick_words(1, 1)
-        w3_raw.extend(load_w3(W3_CHUNK, N, "table1"))
+        w1_raw.append(load_w1(1, "table1"))
         pick_words(2, HALVES)
+        w1_raw.append(load_w1(2, "table2"))
 
         w1_codes = [held(f"w1_codes{a}", [P, H], U32) for a in range(PASSES)]
         w1_planes = [held(f"w1_planes{a}", [P, H], U8) for a in range(PASSES)]
@@ -137,17 +134,23 @@ def tile_list_walnut_lane_scores_kernel(
 
         w3_codes, w3_planes = [], []
 
-        def quantise_w3(c):
+        def round_w3(c):
             rounded = held(f"w3_rounded{c}", [P, PACK * W3_CHUNK], BF16)
             interleave(rounded[:], w3_raw[c], nc.scalar.copy)
-            codes = held(f"w3_codes{c}", [P, W3_CHUNK], U32, tag="table2" if c == 0 else None)
+            return rounded
+
+        def quantise_w3(c, rounded):
+            codes = held(f"w3_codes{c}", [P, W3_CHUNK], U32, tag="w1_dealt0" if c == 0 else None)
             plane = held(f"w3_plane{c}", [P, W3_CHUNK], U8)
             nc.vector.quantize_mx(out=codes[:].bitcast(FP8X4), scales=plane[:], in_=rounded[:])
             w3_codes.append(codes)
             w3_planes.append(plane)
 
-        quantise_w3(0)
+        w3_first = round_w3(0)
+        gains = held("gains", [P, PACK], F32, tag="w3_raw0")
+        nc.sync.dma_start(gains[:], gain.rearrange("(p t) -> p t", t=PACK))
         quantise_w1(0, nc.vector.tensor_copy)
+        quantise_w3(0, w3_first)
 
         banks = {(t, s): psum.tile([P, BANK], F32, name=f"h2_bank{t}{s}", tag="bank") for t in range(PACK) for s in range(HALVES)}
 
@@ -183,15 +186,16 @@ def tile_list_walnut_lane_scores_kernel(
         for t in range(PACK):
             if t >= 2:
                 quantise_w1(t - 1, nc.scalar.copy)
-            h2 = held(f"h2_{t}", [P, S], F32, tag={2: "tab_planes", 3: "table0"}.get(t))
+            h2 = held(f"h2_{t}", [P, S], F32, tag={2: "table1", 3: "table2"}.get(t))
             for s in range(HALVES):
                 nc.scalar.copy(h2[:, s * BANK : (s + 1) * BANK], banks[t, s][:])
             diff = held(f"diff{t}", [P, PAIRS], F32)
-            combine_pairs(h2, diff[:], ALU.subtract, tag="w1_raw0" if t == 0 else None)
+            combine_pairs(h2, diff[:], ALU.subtract, tag="tab_planes" if t == 0 else None)
             for i in range(PACK):
                 nc.sync.dma_start(diff_dealt[32 * t : 32 * (t + 1), i, :], diff[i:P:PACK, :])
 
-        w4_codes = held("w4_codes", [P, N], I32, tag="w1_dealt0")
+        w3_raw.extend(load_w3(W3_CHUNK, N, "tab_planes"))
+        w4_codes = held("w4_codes", [P, N], I32, tag="w3_rounded0")
         nc.sync.dma_start(w4_codes[:], w4_words[0].rearrange("p c i -> p (c i)").bitcast(I32))
         w4_planes = held("w4_planes", [P, N], U8, tag="w1_dealt1")
         nc.vector.memset(w4_planes[:].bitcast(I32), 0)
@@ -266,7 +270,7 @@ def tile_list_walnut_lane_scores_kernel(
             ys[n] = ring.tile([P, PAIRS], F32, name="y", bufs=4, align_bytes=64)
             nc.vector.tensor_tensor(ys[n][:], y1_bank[:], y2[:], ALU.max)
             if at == 0 and (c + 1) * W3_CHUNK < N:
-                quantise_w3(c + 1)
+                quantise_w3(c + 1, round_w3(c + 1))
 
         def pick_lane(n):
             lanes[n] = ring.tile([P, LANES], F32, name="lane", align_bytes=64)

@@ -61,7 +61,7 @@ def tile_list_walnut_lane_scores_kernel(
             return [tile[:, :, c : c + W3_CHUNK] for c in range(0, last - first, W3_CHUNK)]
 
         tab_planes = held("tab_planes", [P, T], U8)
-        nc.gpsimd.memset(tab_planes[:].bitcast(I32), 0)
+        nc.vector.memset(tab_planes[:].bitcast(I32), 0)
         w2_planes = held("w2_planes", [P, PASSES * H], U8)
         nc.vector.memset(w2_planes[:].bitcast(I32), 0)
         table = [load_table(0)]
@@ -69,17 +69,12 @@ def tile_list_walnut_lane_scores_kernel(
         p2 = load_list("p2", pos2)
         p3 = load_list("p3", pos3)
         p4 = load_list("p4", pos4)
-        w3_raw = load_w3(0, W3_CHUNK, None)
         table.append(load_table(1))
-        for q in range(QUADS):
-            nc.gpsimd.dma_start(
-                tab_planes[32 * q : 32 * q + 4 * PASSES, :].bitcast(I32),
-                tab_scales[:, 4 * q : 4 * q + 4, :].bitcast(I32),
-            )
+        w1_raw = [load_w1(0, None)]
         for q in range(QUADS):
             nc.scalar.dma_start(
-                w2_planes[32 * q : 32 * q + 4, :].bitcast(I32).rearrange("r (a c) -> r a c", a=PASSES),
-                w2_scales[:, 4 * q : 4 * q + 4, :].bitcast(I32).rearrange("a r c -> r a c"),
+                tab_planes[32 * q : 32 * q + 4 * PASSES, :].bitcast(I32),
+                tab_scales[:, 4 * q : 4 * q + 4, :].bitcast(I32),
             )
         table.append(load_table(2))
         w2_codes = held("w2_codes", [P, PASSES * 2 * H], U8)
@@ -87,6 +82,11 @@ def tile_list_walnut_lane_scores_kernel(
             w2_codes[:].bitcast(I32).rearrange("p (a c) -> p a c", a=PASSES),
             w2_words.bitcast(I32).rearrange("a p c -> p a c"),
         )
+        for q in range(QUADS):
+            nc.sync.dma_start(
+                w2_planes[32 * q : 32 * q + 4, :].bitcast(I32).rearrange("r (a c) -> r a c", a=PASSES),
+                w2_scales[:, 4 * q : 4 * q + 4, :].bitcast(I32).rearrange("a r c -> r a c"),
+            )
 
         picked = [held(f"picked{a}", [P, S], U32) for a in range(PASSES)]
 
@@ -98,28 +98,27 @@ def tile_list_walnut_lane_scores_kernel(
                     table[a][:].bitcast(U32).indirect(idx[:, s * width // 16 : (s + 1) * width // 16]),
                 )
 
-        picked_planes = held("picked_planes", [P, S], U8)
+        pick_words(0, 1)
+        w1_raw.append(load_w1(1, "table0"))
+        pick_words(1, 1)
+        picked_planes = held("picked_planes", [P, S], U8, tag="table1")
         nc.vector.tensor_copy(picked_planes[:], tab_planes[:].indirect(idx[:]))
         planes = [picked_planes]
         live = 32 * (QUADS - 1) + 4
         for a in range(1, PASSES):
             shifted = held(f"shifted{a}", [P, S], U8)
             nc.vector.memset(shifted[:].bitcast(I32), 0)
-            nc.scalar.dma_start(shifted[0:live, :].bitcast(I32), picked_planes[4 * a : 4 * a + live, :].bitcast(I32))
+            nc.sync.dma_start(shifted[0:live, :].bitcast(I32), picked_planes[4 * a : 4 * a + live, :].bitcast(I32))
             planes.append(shifted)
 
-        w1_raw = [load_w1(0, "tab_planes")]
-        pick_words(0, 1)
-        pick_words(1, 1)
-        w1_raw.append(load_w1(1, "table1"))
+        w1_raw.append(load_w1(2, "tab_planes"))
         pick_words(2, HALVES)
-        w1_raw.append(load_w1(2, "table2"))
 
         w1_codes = [held(f"w1_codes{a}", [P, H], U32) for a in range(PASSES)]
         w1_planes = [held(f"w1_planes{a}", [P, H], U8) for a in range(PASSES)]
 
         def quantise_w1(a, copy):
-            dealt = held(f"w1_dealt{a}", [P, PACK * H], BF16)
+            dealt = held(f"w1_dealt{a}", [P, PACK * H], BF16, tag="table2" if a == 1 else None)
             copy(
                 dealt[:].rearrange("p (t m j) -> p m t j", t=PACK, j=PACK),
                 w1_raw[a][:].rearrange("p j (m t) -> p m t j", t=PACK),
@@ -140,17 +139,17 @@ def tile_list_walnut_lane_scores_kernel(
             return rounded
 
         def quantise_w3(c, rounded):
-            codes = held(f"w3_codes{c}", [P, W3_CHUNK], U32, tag="w1_dealt0" if c == 0 else None)
+            codes = held(f"w3_codes{c}", [P, W3_CHUNK], U32)
             plane = held(f"w3_plane{c}", [P, W3_CHUNK], U8)
             nc.vector.quantize_mx(out=codes[:].bitcast(FP8X4), scales=plane[:], in_=rounded[:])
             w3_codes.append(codes)
             w3_planes.append(plane)
 
-        w3_first = round_w3(0)
-        gains = held("gains", [P, PACK], F32, tag="w3_raw0")
+        quantise_w1(0, nc.scalar.copy)
+        gains = held("gains", [P, PACK], F32, tag="w1_raw0")
         nc.sync.dma_start(gains[:], gain.rearrange("(p t) -> p t", t=PACK))
-        quantise_w1(0, nc.vector.tensor_copy)
-        quantise_w3(0, w3_first)
+        w3_raw = load_w3(0, W3_CHUNK, "w1_dealt0")
+        quantise_w1(1, nc.vector.tensor_copy)
 
         banks = {(t, s): psum.tile([P, BANK], F32, name=f"h2_bank{t}{s}", tag="bank") for t in range(PACK) for s in range(HALVES)}
 
@@ -184,20 +183,21 @@ def tile_list_walnut_lane_scores_kernel(
 
         diff_dealt = held("diff_dealt", [P, PACK, PAIRS], F32)
         for t in range(PACK):
-            if t >= 2:
-                quantise_w1(t - 1, nc.scalar.copy)
-            h2 = held(f"h2_{t}", [P, S], F32, tag={2: "table1", 3: "table2"}.get(t))
+            if t == 2:
+                quantise_w1(2, nc.scalar.copy)
+            h2 = held(f"h2_{t}", [P, S], F32, tag="tab_planes" if t == 2 else None)
             for s in range(HALVES):
                 nc.scalar.copy(h2[:, s * BANK : (s + 1) * BANK], banks[t, s][:])
             diff = held(f"diff{t}", [P, PAIRS], F32)
-            combine_pairs(h2, diff[:], ALU.subtract, tag="tab_planes" if t == 0 else None)
+            combine_pairs(h2, diff[:], ALU.subtract, tag="table0" if t == 0 else None)
             for i in range(PACK):
                 nc.sync.dma_start(diff_dealt[32 * t : 32 * (t + 1), i, :], diff[i:P:PACK, :])
 
-        w3_raw.extend(load_w3(W3_CHUNK, N, "tab_planes"))
+        w3_raw.extend(load_w3(W3_CHUNK, N, "table0"))
+        quantise_w3(0, round_w3(0))
         w4_codes = held("w4_codes", [P, N], I32, tag="w3_rounded0")
         nc.sync.dma_start(w4_codes[:], w4_words[0].rearrange("p c i -> p (c i)").bitcast(I32))
-        w4_planes = held("w4_planes", [P, N], U8, tag="w1_dealt1")
+        w4_planes = held("w4_planes", [P, N], U8, tag="table2")
         nc.vector.memset(w4_planes[:].bitcast(I32), 0)
         for q in range(QUADS):
             nc.sync.dma_start(

@@ -134,12 +134,12 @@ def tile_list_walnut_lane_scores_kernel(
         w3_codes, w3_planes = [], []
 
         def round_w3(c):
-            rounded = held(f"w3_rounded{c}", [P, PACK * W3_CHUNK], BF16)
+            rounded = held(f"w3_rounded{c}", [P, PACK * W3_CHUNK], BF16, tag="diff_dealt" if c == 1 else None)
             interleave(rounded[:], w3_raw[c], nc.scalar.copy)
             return rounded
 
         def quantise_w3(c, rounded):
-            codes = held(f"w3_codes{c}", [P, W3_CHUNK], U32)
+            codes = held(f"w3_codes{c}", [P, W3_CHUNK], U32, tag="z2" if c == 1 else None)
             plane = held(f"w3_plane{c}", [P, W3_CHUNK], U8)
             nc.vector.quantize_mx(out=codes[:].bitcast(FP8X4), scales=plane[:], in_=rounded[:])
             w3_codes.append(codes)
@@ -230,15 +230,19 @@ def tile_list_walnut_lane_scores_kernel(
         z2_plane = held("z2_plane", [P, PAIRS], U8)
         nc.vector.quantize_mx(out=z2_codes[:].bitcast(FP8X4), scales=z2_plane[:], in_=z2[:])
 
+        w3_second = round_w3(1)
+
         z1_codes, z1_planes = [], []
         for s in range(2):
-            z1 = held(f"z1_{s}", [P, PACK * HALF_PAIRS], BF16)
+            z1 = held(f"z1_{s}", [P, PACK * HALF_PAIRS], BF16, tag="z2" if s else None)
             interleave(z1[:], prod[:, :, s * HALF_PAIRS : (s + 1) * HALF_PAIRS], nc.vector.tensor_copy if s else nc.scalar.copy)
             codes = held(f"z1_codes{s}", [P, HALF_PAIRS], U32)
             plane = held(f"z1_plane{s}", [P, HALF_PAIRS], U8)
             nc.vector.quantize_mx(out=codes[:].bitcast(FP8X4), scales=plane[:], in_=z1[:])
             z1_codes.append(codes)
             z1_planes.append(plane)
+
+        quantise_w3(1, w3_second)
 
         ys, lanes = {}, {}
 
@@ -269,8 +273,8 @@ def tile_list_walnut_lane_scores_kernel(
                 )
             ys[n] = ring.tile([P, PAIRS], F32, name="y", bufs=4, align_bytes=64)
             nc.vector.tensor_tensor(ys[n][:], y1_bank[:], y2[:], ALU.max)
-            if at == 0 and (c + 1) * W3_CHUNK < N:
-                quantise_w3(c + 1, round_w3(c + 1))
+            if n == 1:
+                quantise_w3(2, round_w3(2))
 
         def pick_lane(n):
             lanes[n] = ring.tile([P, LANES], F32, name="lane", align_bytes=64)

from contextlib import ExitStack

import concourse.mybir as mybir

K, H, N, T, S, PAIRS, LANES = 1536, 512, 768, 2048, 1024, 512, 256
FLOPS = 2 * (2 * K * H * S + 2 * H * N * PAIRS)

F32 = mybir.dt.float32
BF16 = mybir.dt.bfloat16
I32 = mybir.dt.int32
U32 = mybir.dt.uint32
U16 = mybir.dt.uint16
U8 = mybir.dt.uint8
FP8X4 = mybir.dt.float8_e4m3fn_x4
FP4X4 = mybir.dt.float4_e2m1fn_x4
ACT = mybir.ActivationFunctionType
ALU = mybir.AluOpType

P = 128
PACK = 4
PASSES = K // (P * PACK)
BANK = 512
HALVES = S // BANK
QUADS = 4
N_TILES = N // P
W3_CHUNK = 256
HALF_PAIRS = PAIRS // 2


def tile_list_walnut_lane_scores_kernel(
    tc, tab_words, tab_scales, offs, pos1, pos2, pos3, pos4, w1, w2_words, w2_scales, gain, w3, w4_words, w4_scales, out
):
    nc = tc.nc
    with ExitStack() as ctx:
        keep = ctx.enter_context(tc.tile_pool(name="keep", bufs=1))
        ring = ctx.enter_context(tc.tile_pool(name="ring", bufs=3))
        psum = ctx.enter_context(tc.psum_pool(name="psum", bufs=8))

        def held(name, shape, dtype, tag=None):
            return keep.tile(shape, dtype, name=name, tag=tag or name, align_bytes=64)

        def load_list(name, source):
            tile = keep.tile(list(source.shape), U16, name=name)
            nc.sync.dma_start(tile[:], source)
            return tile

        idx = load_list("idx", offs)
        def load_table(a):
            tile = held(f"table{a}", [P, T], I32)
            nc.sync.dma_start(tile[:], tab_words[a].rearrange("p t i -> p (t i)").bitcast(I32))
            return tile

        def load_w1(a, tag):
            tile = held(f"w1_raw{a}", [P, PACK, H], F32, tag=tag)
            nc.sync.dma_start(tile[:], w1[a * P * PACK : (a + 1) * P * PACK, :].rearrange("(p j) c -> p j c", j=PACK))
            return tile

        def load_w3(first, last, tag):
            tile = held(f"w3_raw{first}", [P, PACK, last - first], F32, tag=tag)
            nc.sync.dma_start(tile[:], w3[:, first:last].rearrange("(p j) c -> p j c", j=PACK))
            return [tile[:, :, c : c + W3_CHUNK] for c in range(0, last - first, W3_CHUNK)]

        tab_planes = held("tab_planes", [P, T], U8)
        nc.vector.memset(tab_planes[:].bitcast(I32), 0)
        w2_planes = held("w2_planes", [P, PASSES * H], U8)
        nc.vector.memset(w2_planes[:].bitcast(I32), 0)
        table = [load_table(0)]
        p1 = load_list("p1", pos1)
        p2 = load_list("p2", pos2)
        p3 = load_list("p3", pos3)
        p4 = load_list("p4", pos4)
        table.append(load_table(1))
        w1_raw = [load_w1(0, None)]
        for q in range(QUADS):
            nc.scalar.dma_start(
                tab_planes[32 * q : 32 * q + 4 * PASSES, :].bitcast(I32),
                tab_scales[:, 4 * q : 4 * q + 4, :].bitcast(I32),
            )
        table.append(load_table(2))
        w2_codes = held("w2_codes", [P, PASSES * 2 * H], U8)
        nc.sync.dma_start(
            w2_codes[:].bitcast(I32).rearrange("p (a c) -> p a c", a=PASSES),
            w2_words.bitcast(I32).rearrange("a p c -> p a c"),
        )
        for q in range(QUADS):
            nc.sync.dma_start(
                w2_planes[32 * q : 32 * q + 4, :].bitcast(I32).rearrange("r (a c) -> r a c", a=PASSES),
                w2_scales[:, 4 * q : 4 * q + 4, :].bitcast(I32).rearrange("a r c -> r a c"),
            )

        picked = [held(f"picked{a}", [P, S], U32) for a in range(PASSES)]

        def pick_words(a, pieces):
            width = S // pieces
            for s in range(pieces):
                nc.vector.tensor_copy(
                    picked[a][:, s * width : (s + 1) * width],
                    table[a][:].bitcast(U32).indirect(idx[:, s * width // 16 : (s + 1) * width // 16]),
                )

        pick_words(0, 1)
        w1_raw.append(load_w1(1, "table0"))
        pick_words(1, 1)
        picked_planes = held("picked_planes", [P, S], U8, tag="table1")
        nc.vector.tensor_copy(picked_planes[:], tab_planes[:].indirect(idx[:]))
        planes = [picked_planes]
        live = 32 * (QUADS - 1) + 4
        for a in range(1, PASSES):
            shifted = held(f"shifted{a}", [P, S], U8)
            nc.vector.memset(shifted[:].bitcast(I32), 0)
            nc.sync.dma_start(shifted[0:live, :].bitcast(I32), picked_planes[4 * a : 4 * a + live, :].bitcast(I32))
            planes.append(shifted)

        w1_raw.append(load_w1(2, "tab_planes"))
        pick_words(2, HALVES)

        w1_codes = [held(f"w1_codes{a}", [P, H], U32) for a in range(PASSES)]
        w1_planes = [held(f"w1_planes{a}", [P, H], U8) for a in range(PASSES)]

        def quantise_w1(a, copy):
            dealt = held(f"w1_dealt{a}", [P, PACK * H], BF16, tag="table2" if a == 1 else None)
            copy(
                dealt[:].rearrange("p (t m j) -> p m t j", t=PACK, j=PACK),
                w1_raw[a][:].rearrange("p j (m t) -> p m t j", t=PACK),
            )
            nc.vector.quantize_mx(out=w1_codes[a][:].bitcast(FP8X4), scales=w1_planes[a][:], in_=dealt[:])

        def interleave(dest, source, copy):
            copy(dest.rearrange("p (c i t) -> p c t i", i=4, t=PACK), source.rearrange("p t (c i) -> p c t i", i=4))

        def scalar_abs(dest, source):
            nc.scalar.activation(dest, source, ACT.Abs)

        w3_codes, w3_planes = [], []

        def round_w3(c):
            rounded = held(f"w3_rounded{c}", [P, PACK * W3_CHUNK], BF16, tag="diff_dealt" if c == 1 else None)
            interleave(rounded[:], w3_raw[c], nc.scalar.copy)
            return rounded

        def quantise_w3(c, rounded):
            codes = held(f"w3_codes{c}", [P, W3_CHUNK], U32, tag="z2" if c == 1 else None)
            plane = held(f"w3_plane{c}", [P, W3_CHUNK], U8)
            nc.vector.quantize_mx(out=codes[:].bitcast(FP8X4), scales=plane[:], in_=rounded[:])
            w3_codes.append(codes)
            w3_planes.append(plane)

        quantise_w1(0, nc.scalar.copy)
        gains = held("gains", [P, PACK], F32, tag="w1_raw0")
        nc.sync.dma_start(gains[:], gain.rearrange("(p t) -> p t", t=PACK))
        w3_raw = load_w3(0, W3_CHUNK, "w1_dealt0")
        quantise_w1(1, nc.vector.tensor_copy)

        banks = {(t, s): psum.tile([P, BANK], F32, name=f"h2_bank{t}{s}", tag="bank") for t in range(PACK) for s in range(HALVES)}

        def h2_passes(t, passes):
            for a in passes:
                for s in range(HALVES):
                    first = a * H + t * P
                    nc.tensor.matmul_mx(
                        out=banks[t, s][:],
                        lhsT=w2_codes[:, 2 * first : 2 * (first + P)].bitcast(FP4X4),
                        lhsT_scale=w2_planes[:, first : first + P],
                        rhs=picked[a][:, s * BANK : (s + 1) * BANK].bitcast(FP8X4),
                        rhs_scale=planes[a][:, s * BANK : (s + 1) * BANK],
                        start=(a == 0),
                        stop=(a == PASSES - 1),
                    )

        for t in range(PACK):
            h2_passes(t, range(PASSES))

        def combine_pairs(h, dest, op, tag=None):
            if tag:
                second = held("first_second", [P, PAIRS], F32, tag=tag)
            else:
                second = ring.tile([P, PAIRS], F32, name="second", align_bytes=64)
            pieces = [(slice(m, m + HALF_PAIRS), slice(m // 16, (m + HALF_PAIRS) // 16)) for m in (0, HALF_PAIRS)]
            for pairs, cols in pieces:
                nc.vector.tensor_copy(second[:, pairs], h[:].indirect(p2[:, cols]))
            for pairs, cols in pieces:
                nc.vector.tensor_tensor(dest[:, pairs], h[:].indirect(p1[:, cols]), second[:, pairs], op)

        diff_dealt = held("diff_dealt", [P, PACK, PAIRS], F32)
        for t in range(PACK):
            if t == 2:
                quantise_w1(2, nc.scalar.copy)
            h2 = held(f"h2_{t}", [P, S], F32, tag="tab_planes" if t == 2 else None)
            for s in range(HALVES):
                nc.scalar.copy(h2[:, s * BANK : (s + 1) * BANK], banks[t, s][:])
            diff = held(f"diff{t}", [P, PAIRS], F32)
            combine_pairs(h2, diff[:], ALU.subtract, tag="table0" if t == 0 else None)
            for i in range(PACK):
                nc.sync.dma_start(diff_dealt[32 * t : 32 * (t + 1), i, :], diff[i:P:PACK, :])

        w3_raw.extend(load_w3(W3_CHUNK, N, "table0"))
        quantise_w3(0, round_w3(0))
        w4_codes = held("w4_codes", [P, N], I32, tag="w3_rounded0")
        nc.sync.dma_start(w4_codes[:], w4_words[0].rearrange("p c i -> p (c i)").bitcast(I32))
        w4_planes = held("w4_planes", [P, N], U8, tag="table2")
        nc.vector.memset(w4_planes[:].bitcast(I32), 0)
        for q in range(QUADS):
            nc.sync.dma_start(
                w4_planes[32 * q : 32 * q + 4, :].bitcast(I32), w4_scales[0, 4 * q : 4 * q + 4, :].bitcast(I32)
            )

        prod = held("prod", [P, PACK, PAIRS], F32)
        for t in range(PACK):
            bent = ring.tile([P, S], F32, name="bent", bufs=2, align_bytes=64)
            for s in range(HALVES):
                bank = psum.tile([P, BANK], F32, name="h1_bank", tag="bank")
                for a in range(PASSES):
                    nc.tensor.matmul_mx(
                        out=bank[:],
                        lhsT=w1_codes[a][:, t * P : (t + 1) * P].bitcast(FP8X4),
                        lhsT_scale=w1_planes[a][:, t * P : (t + 1) * P],
                        rhs=picked[a][:, s * BANK : (s + 1) * BANK].bitcast(FP8X4),
                        rhs_scale=planes[a][:, s * BANK : (s + 1) * BANK],
                        start=(a == 0),
                        stop=(a == PASSES - 1),
                    )
                nc.scalar.activation(bent[:, s * BANK : (s + 1) * BANK], bank[:], ACT.Tanh)
            h1 = held(f"h1_{t}", [P, S], F32)
            nc.scalar.activation(h1[:], bent[:], ACT.Copy, scale=gains[:, t : t + 1])
            combine_pairs(h1, prod[:, t, :], ALU.mult)

        z2 = held("z2", [P, PACK * PAIRS], BF16)
        interleave(z2[:], diff_dealt[:], scalar_abs)
        z2_codes = held("z2_codes", [P, PAIRS], U32)
        z2_plane = held("z2_plane", [P, PAIRS], U8)
        nc.vector.quantize_mx(out=z2_codes[:].bitcast(FP8X4), scales=z2_plane[:], in_=z2[:])

        w3_second = round_w3(1)

        z1_codes, z1_planes = [], []
        for s in range(2):
            z1 = held(f"z1_{s}", [P, PACK * HALF_PAIRS], BF16, tag="z2" if s else None)
            interleave(z1[:], prod[:, :, s * HALF_PAIRS : (s + 1) * HALF_PAIRS], nc.vector.tensor_copy if s else nc.scalar.copy)
            codes = held(f"z1_codes{s}", [P, HALF_PAIRS], U32)
            plane = held(f"z1_plane{s}", [P, HALF_PAIRS], U8)
            nc.vector.quantize_mx(out=codes[:].bitcast(FP8X4), scales=plane[:], in_=z1[:])
            z1_codes.append(codes)
            z1_planes.append(plane)

        quantise_w3(1, w3_second)

        ys, lanes = {}, {}

        def score_views(n):
            c, at = divmod(n * P, W3_CHUNK)
            y2_bank = psum.tile([P, PAIRS], F32, name="y2_bank", tag="bank")
            nc.tensor.matmul_mx(
                out=y2_bank[:],
                lhsT=w4_codes[:, n * P : (n + 1) * P].bitcast(FP8X4),
                lhsT_scale=w4_planes[:, n * P : (n + 1) * P],
                rhs=z2_codes[:].bitcast(FP8X4),
                rhs_scale=z2_plane[:],
                start=True,
                stop=True,
            )
            y2 = ring.tile([P, PAIRS], F32, name="y2", align_bytes=64)
            nc.scalar.copy(y2[:], y2_bank[:])
            y1_bank = psum.tile([P, PAIRS], F32, name="y1_bank", tag="bank")
            for s in range(2):
                nc.tensor.matmul_mx(
                    out=y1_bank[:, s * HALF_PAIRS : (s + 1) * HALF_PAIRS],
                    lhsT=w3_codes[c][:, at : at + P].bitcast(FP8X4),
                    lhsT_scale=w3_planes[c][:, at : at + P],
                    rhs=z1_codes[s][:].bitcast(FP8X4),
                    rhs_scale=z1_planes[s][:],
                    start=True,
                    stop=True,
                )
            ys[n] = ring.tile([P, PAIRS], F32, name="y", bufs=4, align_bytes=64)
            nc.vector.tensor_tensor(ys[n][:], y1_bank[:], y2[:], ALU.max)
            if n == 1:
                quantise_w3(2, round_w3(2))

        def pick_lane(n):
            lanes[n] = ring.tile([P, LANES], F32, name="lane", align_bytes=64)
            nc.vector.tensor_copy(lanes[n][:], ys[n][:].indirect(p4[:]))

        def pair_lanes(n):
            scores = ring.tile([P, LANES], F32, name="scores", bufs=N_TILES, align_bytes=64)
            nc.vector.tensor_tensor(scores[:], ys[n][:].indirect(p3[:]), lanes[n][:], ALU.mult)
            nc.sync.dma_start(out[n * P : (n + 1) * P, :], scores[:])

        for step in range(N_TILES + 2):
            for lag, stage in enumerate((score_views, pick_lane, pair_lanes)):
                if 0 <= step - lag < N_TILES:
                    stage(step - lag)
